import numpy as np, ml_dtypes
CORES = [65,73,81,89,97,105,113,121]
N = 8
TK = 128
def setup_inputs(rng):
    return {"b": rng.standard_normal((N, 128, TK), dtype=np.float32).astype(ml_dtypes.bfloat16), "l": (rng.standard_normal((N, 128, N * 128), dtype=np.float32) / 16).astype(ml_dtypes.bfloat16)}
def setup_inputs_big(rng):
    d = setup_inputs(rng)
    for k in ("b",): d[k] = (d[k].astype(np.float32) * 1048576.0).astype(d[k].dtype)
    return d
def setup_inputs_small(rng):
    d = setup_inputs(rng)
    for k in ("b",): d[k] = (d[k].astype(np.float32) * (1 / 1048576.0)).astype(d[k].dtype)
    return d
def setup_inputs_apart(rng):
    d = setup_inputs(rng)
    f = (10.0 ** rng.permutation(np.linspace(-1.5, 1.5, N))).astype(np.float32).reshape(N, 1, 1)
    for k in ("b",): d[k] = (d[k].astype(np.float32) * f).astype(d[k].dtype)
    return d
def reference(b, l):
    B, L = b.astype(np.float64), l.astype(np.float64)
    y = np.zeros((N, 128, TK))
    for r in range(N):
        acc = B[r].copy()
        for s in range(r):
            acc -= L[r][:, 128 * s:128 * s + 128].T @ y[s]
        y[r] = acc
    return {"y": y.astype(ml_dtypes.bfloat16)}

@@ -1,0 +1,202 @@
+from concourse.bass import DstId, RemoteDMATransfer
+from concourse.mybir import AluOpType
+
+N = 8
+TK = 128
+NCH = [1, 1, 2, 2, 4, 4, 4, 1]
+NFEED = [4, 4, 8, 8, 8, 8, 8, 0]
+LATE = 4.0
+VEC = 2.5
+
+SCRATCH = {"yb": ("sbuf", [128, N * TK], "bfloat16")}
+for _q in range(N):
+    SCRATCH["in%d" % _q] = ("sbuf", [128, (_q + 1) * TK], "bfloat16")
+    if _q < N - 1:
+        SCRATCH["st%d" % _q] = ("dram", [NCH[_q], 128, (_q + 1) * TK // NCH[_q]], "bfloat16")
+    if _q > 0:
+        SCRATCH["ps%d" % _q] = ("psum", [128, 512], "float32")
+
+SEMAPHORES = (["ld", "own", "fed", "snt", "yv", "sto"] + ["a%d" % q for q in range(N - 1)]
+              + ["m%d" % r for r in range(1, N)])
+
+
+def _bits(mask):
+    return [i for i in range(mask.bit_length()) if (mask >> i) & 1]
+
+
+def _mk(bits):
+    m = 0
+    for b in bits:
+        m |= 1 << b
+    return m
+
+
+def _and_masks(topo, src, dsts):
+    m = topo.mask(src, dsts[0])
+    for d in dsts[1:]:
+        m &= topo.mask(src, d)
+    return m
+
+
+def _plan(T, topo):
+    cores = list(T.cores)
+    plan = []
+    for q in range(N):
+        c = cores[q]
+        later = list(range(N - 1, q, -1))
+        direct = [d for d in later if topo.may_write(c, cores[d])]
+        cross = [d for d in later if d not in direct]
+        relays = []
+        if cross:
+            cand = [x for x in range(topo.CORES_PER_CHIP * topo.CHIPS)
+                    if topo.chip(x) == topo.chip(c) and x not in cores
+                    and all(topo.may_write(x, cores[d]) for d in cross)]
+            same = [x for x in cand if topo.die(x) == topo.die(c)]
+            other = [x for x in cand if topo.die(x) != topo.die(c)]
+            mixed = []
+            for i in range(max(len(same), len(other))):
+                mixed += same[i:i + 1] + other[i:i + 1]
+            relays = mixed[:NCH[q]]
+        plan.append({"direct": direct, "cross": cross, "relays": relays})
+    return plan
+
+
+def _dst(topo, c):
+    rid, pid, _se = topo.addr(c)
+    return DstId(rid=rid, pnc=pid)
+
+
+def _order(R, arr):
+    ready = {0: arr[0]}
+    todo = [(r, s) for r in range(1, R + 1) for s in range(r)]
+    left = {r: r for r in range(1, R + 1)}
+    t, order = 0.0, []
+    while todo:
+        can = [p for p in todo if p[1] in ready]
+        now = [p for p in can if max(arr[p[0]], ready[p[1]]) <= t]
+        if not now:
+            t = min(max(arr[p[0]], ready[p[1]]) for p in can)
+            continue
+        p = min(now)
+        todo.remove(p)
+        order.append(p)
+        t += 1.0
+        left[p[0]] -= 1
+        if left[p[0]] == 0:
+            ready[p[0]] = t + VEC
+    return order
+
+
+def _relay(g, core, T, topo, q, j, cross):
+    cores = list(T.cores)
+    wc = (q + 1) * TK // NCH[q]
+    dsts = [cores[d] for d in cross]
+    mask = _and_masks(topo, core, dsts)
+    g.wait_ge(T.sem.fed, NFEED[q] // NCH[q])
+    g.remote_dma_fused([RemoteDMATransfer(
+        dst_ids=[_dst(topo, c) for c in dsts], dma_engine_mask=mask, remote_sem=T.sem["a%d" % q],
+        srcs=[T["st%d" % q][j]], dsts=[T["in%d" % q][:, j * wc:(j + 1) * wc] for _c in dsts])],
+        local_sem=T.sem.snt)
+    g.wait_ge(T.sem.snt, len(_bits(mask)))
+
+
+def rank_program(g, core, T, topo):
+    plan = _plan(T, topo)
+    cores = list(T.cores)
+    q = T.rank_of(core)
+    if q is None:
+        for s in range(N):
+            if core in plan[s]["relays"]:
+                _relay(g, core, T, topo, s, plan[s]["relays"].index(core), plan[s]["cross"])
+        return
+
+    me = plan[q]
+    relays, direct = me["relays"], me["direct"]
+    c = len(relays)
+    w = (q + 1) * TK
+    queues = [g.sync, g.scalar]
+
+    nld = 0
+    if c:
+        st = T["st%d" % q]
+        wc = w // c
+        for j in range(c):
+            lo, hi = j * wc, (j + 1) * wc
+            if lo < TK:
+                e = min(hi, TK)
+                queues[nld % 2].dma_start(st[j, :, 0:e - lo], T.b[:, lo:e]).then_inc(T.sem.ld, 16)
+                nld += 1
+            if hi > TK:
+                s0 = max(lo, TK)
+                queues[nld % 2].dma_start(st[j, :, s0 - lo:wc], T.l[:, s0 - TK:hi - TK]).then_inc(T.sem.ld, 16)
+                nld += 1
+    if q == 0:
+        g.scalar.dma_start(T.y[:], T.b[:]).then_inc(T.sem.sto, 16)
+        g.scalar.wait_ge(T.sem.sto, 16)
+    else:
+        g.sync.dma_start(T["in%d" % q][:, 0:TK], T.b[:]).then_inc(T.sem.own, 16)
+        g.scalar.dma_start(T["in%d" % q][:, TK:w], T.l[:, 0:w - TK]).then_inc(T.sem.own, 16)
+
+    sent = 0
+    if c:
+        g.wait_ge(T.sem.ld, 16 * nld)
+        on = _and_masks(topo, core, relays)
+        off = topo.mask(core, cores[N - 1])
+        eng = (_bits(on & ~off) + _bits(on & off))[:NFEED[q]]
+        g.remote_dma_fused([RemoteDMATransfer(
+            dst_ids=[_dst(topo, relays[j])], dma_engine_mask=_mk(eng[j::c]), remote_sem=T.sem.fed,
+            srcs=[T["st%d" % q][j]], dsts=[T["st%d" % q][j]]) for j in range(c)], local_sem=T.sem.snt)
+        sent += len(eng)
+    if direct:
+        if c == 1:
+            src = T["st%d" % q][0]
+        else:
+            g.wait_ge(T.sem.own, 32)
+            src = T["in%d" % q][:]
+        dsts = [cores[d] for d in direct]
+        mask = _and_masks(topo, core, dsts)
+        g.remote_dma_fused([RemoteDMATransfer(
+            dst_ids=[_dst(topo, x) for x in dsts], dma_engine_mask=mask, remote_sem=T.sem["a%d" % q],
+            srcs=[src], dsts=[T["in%d" % q][:] for _x in dsts])], local_sem=T.sem.snt)
+        sent += len(_bits(mask))
+    if sent:
+        g.wait_ge(T.sem.snt, sent)
+    if q == 0:
+        return
+
+    R = q
+
+    def arrival(r):
+        if r == R:
+            return T.sem.own, 32
+        p = plan[r]
+        if R in p["direct"]:
+            return T.sem["a%d" % r], len(_bits(_and_masks(topo, cores[r], [cores[d] for d in p["direct"]])))
+        return T.sem["a%d" % r], sum(len(_bits(_and_masks(topo, x, [cores[d] for d in p["cross"]])))
+                                     for x in p["relays"])
+
+    late = [r for r in range(R) if R in plan[r]["cross"]]
+    arr = {r: (LATE * (r - late[0]) if r in late else 0.0) for r in range(R + 1)}
+    have, ywait, done = [], 0, {r: 0 for r in range(1, R + 1)}
+    for (r, s) in _order(R, arr):
+        for x in (r, 0):
+            if x not in have:
+                sem, n = arrival(x)
+                g.tensor.wait_ge(sem, n)
+                have.append(x)
+        if s > ywait:
+            g.tensor.wait_ge(T.sem.yv, s)
+            ywait = s
+        rhs = T.in0[:] if s == 0 else T.yb[:, s * TK:(s + 1) * TK]
+        g.tensor.matmul(T["ps%d" % r][:, 0:TK], T["in%d" % r][:, (s + 1) * TK:(s + 2) * TK], rhs,
+                        start=(done[r] == 0), stop=(done[r] == r - 1)).then_inc(T.sem["m%d" % r], 1)
+        done[r] += 1
+    for r in range(1, R + 1):
+        sem, n = arrival(r)
+        g.vector.wait_ge(sem, n)
+        g.vector.wait_ge(T.sem["m%d" % r], r)
+        g.vector.tensor_tensor(T.yb[:, r * TK:(r + 1) * TK], T["in%d" % r][:, 0:TK], T["ps%d" % r][:, 0:TK],
+                               AluOpType.subtract).then_inc(T.sem.yv, 1)
+    g.sync.wait_ge(T.sem.yv, R)
+    g.sync.dma_start(T.y[:], T.yb[:, R * TK:(R + 1) * TK]).then_inc(T.sem.sto, 16)
+    g.sync.wait_ge(T.sem.sto, 16)

@@ -3,21 +3,23 @@ from concourse.mybir import AluOpType
 
 N = 8
 TK = 128
-NCH = [1, 1, 2, 2, 4, 4, 4, 1]
+WIDE = 3
+NCH = [1, 1, 2, 4, 4, 4, 4, 1]
 NFEED = [4, 4, 8, 8, 8, 8, 8, 0]
-LATE = 4.0
-VEC = 2.5
+NHF = 2
+CW = TK // NHF
+WIN = 8 // NHF - 1
 
 SCRATCH = {"yb": ("sbuf", [128, N * TK], "bfloat16")}
 for _q in range(N):
     SCRATCH["in%d" % _q] = ("sbuf", [128, (_q + 1) * TK], "bfloat16")
     if _q < N - 1:
         SCRATCH["st%d" % _q] = ("dram", [NCH[_q], 128, (_q + 1) * TK // NCH[_q]], "bfloat16")
-    if _q > 0:
-        SCRATCH["ps%d" % _q] = ("psum", [128, 512], "float32")
+    SCRATCH["ps%d" % _q] = ("psum", [128, 512], "float32")
 
-SEMAPHORES = (["ld", "own", "fed", "snt", "yv", "sto"] + ["a%d" % q for q in range(N - 1)]
-              + ["m%d" % r for r in range(1, N)])
+SEMAPHORES = (["ld", "own", "fed", "snt", "yv"] + ["sto%d" % h for h in range(NHF)]
+              + ["a%d" % q for q in range(N - 1)]
+              + ["m%d" % (r * NHF + h) for r in range(1, N) for h in range(NHF)])
 
 
 def _bits(mask):
@@ -44,7 +46,7 @@ def _plan(T, topo):
     for q in range(N):
         c = cores[q]
         later = list(range(N - 1, q, -1))
-        direct = [d for d in later if topo.may_write(c, cores[d])]
+        direct = [d for d in later if topo.may_write(c, cores[d]) and q < WIDE]
         cross = [d for d in later if d not in direct]
         relays = []
         if cross:
@@ -55,7 +57,7 @@ def _plan(T, topo):
             other = [x for x in cand if topo.die(x) != topo.die(c)]
             mixed = []
             for i in range(max(len(same), len(other))):
-                mixed += same[i:i + 1] + other[i:i + 1]
+                mixed += other[i:i + 1] + same[i:i + 1]
             relays = mixed[:NCH[q]]
         plan.append({"direct": direct, "cross": cross, "relays": relays})
     return plan
@@ -66,24 +68,22 @@ def _dst(topo, c):
     return DstId(rid=rid, pnc=pid)
 
 
-def _order(R, arr):
-    ready = {0: arr[0]}
-    todo = [(r, s) for r in range(1, R + 1) for s in range(r)]
-    left = {r: r for r in range(1, R + 1)}
-    t, order = 0.0, []
-    while todo:
-        can = [p for p in todo if p[1] in ready]
-        now = [p for p in can if max(arr[p[0]], ready[p[1]]) <= t]
-        if not now:
-            t = min(max(arr[p[0]], ready[p[1]]) for p in can)
-            continue
-        p = min(now)
-        todo.remove(p)
-        order.append(p)
-        t += 1.0
-        left[p[0]] -= 1
-        if left[p[0]] == 0:
-            ready[p[0]] = t + VEC
+def _order(R, early):
+    order = []
+
+    def put(r, s):
+        if (r, s, 0) not in order:
+            order.extend([(r, s, h) for h in range(NHF)])
+
+    if 0 in early:
+        for r in range(1, R + 1):
+            if r in early:
+                put(r, 0)
+    for r in range(1, R):
+        for s in range(r):
+            put(r, s)
+        put(R, r - 1)
+    put(R, R - 1)
     return order
 
 
@@ -131,8 +131,8 @@ def rank_program(g, core, T, topo):
                 queues[nld % 2].dma_start(st[j, :, s0 - lo:wc], T.l[:, s0 - TK:hi - TK]).then_inc(T.sem.ld, 16)
                 nld += 1
     if q == 0:
-        g.scalar.dma_start(T.y[:], T.b[:]).then_inc(T.sem.sto, 16)
-        g.scalar.wait_ge(T.sem.sto, 16)
+        g.scalar.dma_start(T.y[:], T.b[:]).then_inc(T.sem.sto0, 16)
+        g.scalar.wait_ge(T.sem.sto0, 16)
     else:
         g.sync.dma_start(T["in%d" % q][:, 0:TK], T.b[:]).then_inc(T.sem.own, 16)
         g.scalar.dma_start(T["in%d" % q][:, TK:w], T.l[:, 0:w - TK]).then_inc(T.sem.own, 16)
@@ -175,28 +175,44 @@ def rank_program(g, core, T, topo):
         return T.sem["a%d" % r], sum(len(_bits(_and_masks(topo, x, [cores[d] for d in p["cross"]])))
                                      for x in p["relays"])
 
-    late = [r for r in range(R) if R in plan[r]["cross"]]
-    arr = {r: (LATE * (r - late[0]) if r in late else 0.0) for r in range(R + 1)}
-    have, ywait, done = [], 0, {r: 0 for r in range(1, R + 1)}
-    for (r, s) in _order(R, arr):
+    def bank(r, h):
+        k = WIN if r == R else (r - 1) % WIN
+        return T["ps%d" % (k * NHF + h)][:, 0:CW]
+
+    def nth(r, h):
+        return (r - 1) * NHF + h + 1
+
+    early = [r for r in range(R + 1) if r == R or R in plan[r]["direct"]]
+    have, ywait, done = [], 0, {(r, h): 0 for r in range(1, R + 1) for h in range(NHF)}
+    for (r, s, h) in _order(R, early):
         for x in (r, 0):
             if x not in have:
                 sem, n = arrival(x)
                 g.tensor.wait_ge(sem, n)
                 have.append(x)
-        if s > ywait:
-            g.tensor.wait_ge(T.sem.yv, s)
-            ywait = s
-        rhs = T.in0[:] if s == 0 else T.yb[:, s * TK:(s + 1) * TK]
-        g.tensor.matmul(T["ps%d" % r][:, 0:TK], T["in%d" % r][:, (s + 1) * TK:(s + 2) * TK], rhs,
-                        start=(done[r] == 0), stop=(done[r] == r - 1)).then_inc(T.sem["m%d" % r], 1)
-        done[r] += 1
+        need = nth(s, h) if s > 0 else 0
+        if done[(r, h)] == 0 and r != R and r > WIN:
+            need = max(need, nth(r - WIN, h))
+        if need > ywait:
+            g.tensor.wait_ge(T.sem.yv, need)
+            ywait = need
+        rhs = (T.in0 if s == 0 else T.yb)[:, s * TK + h * CW:s * TK + (h + 1) * CW]
+        g.tensor.matmul(bank(r, h), T["in%d" % r][:, (s + 1) * TK:(s + 2) * TK], rhs,
+                        start=(done[(r, h)] == 0), stop=(done[(r, h)] == r - 1)).then_inc(
+                            T.sem["m%d" % (r * NHF + h)], 1)
+        done[(r, h)] += 1
     for r in range(1, R + 1):
         sem, n = arrival(r)
         g.vector.wait_ge(sem, n)
-        g.vector.wait_ge(T.sem["m%d" % r], r)
-        g.vector.tensor_tensor(T.yb[:, r * TK:(r + 1) * TK], T["in%d" % r][:, 0:TK], T["ps%d" % r][:, 0:TK],
-                               AluOpType.subtract).then_inc(T.sem.yv, 1)
-    g.sync.wait_ge(T.sem.yv, R)
-    g.sync.dma_start(T.y[:], T.yb[:, R * TK:(R + 1) * TK]).then_inc(T.sem.sto, 16)
-    g.sync.wait_ge(T.sem.sto, 16)
+        for h in range(NHF):
+            g.vector.wait_ge(T.sem["m%d" % (r * NHF + h)], r)
+            g.vector.tensor_tensor(T.yb[:, r * TK + h * CW:r * TK + (h + 1) * CW],
+                                   T["in%d" % r][:, h * CW:(h + 1) * CW], bank(r, h),
+                                   AluOpType.subtract).then_inc(T.sem.yv, 1)
+    for h in range(NHF):
+        qu = queues[h % 2]
+        qu.wait_ge(T.sem.yv, nth(R, h))
+        qu.dma_start(T.y[:, h * CW:(h + 1) * CW],
+                     T.yb[:, R * TK + h * CW:R * TK + (h + 1) * CW]).then_inc(T.sem["sto%d" % h], 16)
+    for h in range(NHF):
+        queues[h % 2].wait_ge(T.sem["sto%d" % h], 16)

from concourse.bass import DstId, RemoteDMATransfer
from concourse.mybir import AluOpType

N = 8
TK = 128
WIDE = 3
NCH = [1, 1, 2, 4, 4, 4, 4, 1]
NFEED = [4, 4, 8, 8, 8, 8, 8, 0]
NHF = 2
CW = TK // NHF
WIN = 8 // NHF - 1

SCRATCH = {"yb": ("sbuf", [128, N * TK], "bfloat16")}
for _q in range(N):
    SCRATCH["in%d" % _q] = ("sbuf", [128, (_q + 1) * TK], "bfloat16")
    if _q < N - 1:
        SCRATCH["st%d" % _q] = ("dram", [NCH[_q], 128, (_q + 1) * TK // NCH[_q]], "bfloat16")
    SCRATCH["ps%d" % _q] = ("psum", [128, 512], "float32")

SEMAPHORES = (["ld", "own", "fed", "snt", "yv"] + ["sto%d" % h for h in range(NHF)]
              + ["a%d" % q for q in range(N - 1)]
              + ["m%d" % (r * NHF + h) for r in range(1, N) for h in range(NHF)])


def _bits(mask):
    return [i for i in range(mask.bit_length()) if (mask >> i) & 1]


def _mk(bits):
    m = 0
    for b in bits:
        m |= 1 << b
    return m


def _and_masks(topo, src, dsts):
    m = topo.mask(src, dsts[0])
    for d in dsts[1:]:
        m &= topo.mask(src, d)
    return m


def _plan(T, topo):
    cores = list(T.cores)
    plan = []
    for q in range(N):
        c = cores[q]
        later = list(range(N - 1, q, -1))
        direct = [d for d in later if topo.may_write(c, cores[d]) and q < WIDE]
        cross = [d for d in later if d not in direct]
        relays = []
        if cross:
            cand = [x for x in range(topo.CORES_PER_CHIP * topo.CHIPS)
                    if topo.chip(x) == topo.chip(c) and x not in cores
                    and all(topo.may_write(x, cores[d]) for d in cross)]
            same = [x for x in cand if topo.die(x) == topo.die(c)]
            other = [x for x in cand if topo.die(x) != topo.die(c)]
            mixed = []
            for i in range(max(len(same), len(other))):
                mixed += other[i:i + 1] + same[i:i + 1]
            relays = mixed[:NCH[q]]
        plan.append({"direct": direct, "cross": cross, "relays": relays})
    return plan


def _dst(topo, c):
    rid, pid, _se = topo.addr(c)
    return DstId(rid=rid, pnc=pid)


def _order(R, early):
    order = []

    def put(r, s):
        if (r, s, 0) not in order:
            order.extend([(r, s, h) for h in range(NHF)])

    if 0 in early:
        for r in range(1, R + 1):
            if r in early:
                put(r, 0)
    for r in range(1, R):
        for s in range(r):
            put(r, s)
        put(R, r - 1)
    put(R, R - 1)
    return order


def _relay(g, core, T, topo, q, j, cross):
    cores = list(T.cores)
    wc = (q + 1) * TK // NCH[q]
    dsts = [cores[d] for d in cross]
    mask = _and_masks(topo, core, dsts)
    g.wait_ge(T.sem.fed, NFEED[q] // NCH[q])
    g.remote_dma_fused([RemoteDMATransfer(
        dst_ids=[_dst(topo, c) for c in dsts], dma_engine_mask=mask, remote_sem=T.sem["a%d" % q],
        srcs=[T["st%d" % q][j]], dsts=[T["in%d" % q][:, j * wc:(j + 1) * wc] for _c in dsts])],
        local_sem=T.sem.snt)
    g.wait_ge(T.sem.snt, len(_bits(mask)))


def rank_program(g, core, T, topo):
    plan = _plan(T, topo)
    cores = list(T.cores)
    q = T.rank_of(core)
    if q is None:
        for s in range(N):
            if core in plan[s]["relays"]:
                _relay(g, core, T, topo, s, plan[s]["relays"].index(core), plan[s]["cross"])
        return

    me = plan[q]
    relays, direct = me["relays"], me["direct"]
    c = len(relays)
    w = (q + 1) * TK
    queues = [g.sync, g.scalar]

    nld = 0
    if c:
        st = T["st%d" % q]
        wc = w // c
        for j in range(c):
            lo, hi = j * wc, (j + 1) * wc
            if lo < TK:
                e = min(hi, TK)
                queues[nld % 2].dma_start(st[j, :, 0:e - lo], T.b[:, lo:e]).then_inc(T.sem.ld, 16)
                nld += 1
            if hi > TK:
                s0 = max(lo, TK)
                queues[nld % 2].dma_start(st[j, :, s0 - lo:wc], T.l[:, s0 - TK:hi - TK]).then_inc(T.sem.ld, 16)
                nld += 1
    if q == 0:
        g.scalar.dma_start(T.y[:], T.b[:]).then_inc(T.sem.sto0, 16)
        g.scalar.wait_ge(T.sem.sto0, 16)
    else:
        g.sync.dma_start(T["in%d" % q][:, 0:TK], T.b[:]).then_inc(T.sem.own, 16)
        g.scalar.dma_start(T["in%d" % q][:, TK:w], T.l[:, 0:w - TK]).then_inc(T.sem.own, 16)

    sent = 0
    if c:
        g.wait_ge(T.sem.ld, 16 * nld)
        on = _and_masks(topo, core, relays)
        off = topo.mask(core, cores[N - 1])
        eng = (_bits(on & ~off) + _bits(on & off))[:NFEED[q]]
        g.remote_dma_fused([RemoteDMATransfer(
            dst_ids=[_dst(topo, relays[j])], dma_engine_mask=_mk(eng[j::c]), remote_sem=T.sem.fed,
            srcs=[T["st%d" % q][j]], dsts=[T["st%d" % q][j]]) for j in range(c)], local_sem=T.sem.snt)
        sent += len(eng)
    if direct:
        if c == 1:
            src = T["st%d" % q][0]
        else:
            g.wait_ge(T.sem.own, 32)
            src = T["in%d" % q][:]
        dsts = [cores[d] for d in direct]
        mask = _and_masks(topo, core, dsts)
        g.remote_dma_fused([RemoteDMATransfer(
            dst_ids=[_dst(topo, x) for x in dsts], dma_engine_mask=mask, remote_sem=T.sem["a%d" % q],
            srcs=[src], dsts=[T["in%d" % q][:] for _x in dsts])], local_sem=T.sem.snt)
        sent += len(_bits(mask))
    if sent:
        g.wait_ge(T.sem.snt, sent)
    if q == 0:
        return

    R = q

    def arrival(r):
        if r == R:
            return T.sem.own, 32
        p = plan[r]
        if R in p["direct"]:
            return T.sem["a%d" % r], len(_bits(_and_masks(topo, cores[r], [cores[d] for d in p["direct"]])))
        return T.sem["a%d" % r], sum(len(_bits(_and_masks(topo, x, [cores[d] for d in p["cross"]])))
                                     for x in p["relays"])

    def bank(r, h):
        k = WIN if r == R else (r - 1) % WIN
        return T["ps%d" % (k * NHF + h)][:, 0:CW]

    def nth(r, h):
        return (r - 1) * NHF + h + 1

    early = [r for r in range(R + 1) if r == R or R in plan[r]["direct"]]
    have, ywait, done = [], 0, {(r, h): 0 for r in range(1, R + 1) for h in range(NHF)}
    for (r, s, h) in _order(R, early):
        for x in (r, 0):
            if x not in have:
                sem, n = arrival(x)
                g.tensor.wait_ge(sem, n)
                have.append(x)
        need = nth(s, h) if s > 0 else 0
        if done[(r, h)] == 0 and r != R and r > WIN:
            need = max(need, nth(r - WIN, h))
        if need > ywait:
            g.tensor.wait_ge(T.sem.yv, need)
            ywait = need
        rhs = (T.in0 if s == 0 else T.yb)[:, s * TK + h * CW:s * TK + (h + 1) * CW]
        g.tensor.matmul(bank(r, h), T["in%d" % r][:, (s + 1) * TK:(s + 2) * TK], rhs,
                        start=(done[(r, h)] == 0), stop=(done[(r, h)] == r - 1)).then_inc(
                            T.sem["m%d" % (r * NHF + h)], 1)
        done[(r, h)] += 1
    for r in range(1, R + 1):
        sem, n = arrival(r)
        g.vector.wait_ge(sem, n)
        for h in range(NHF):
            g.vector.wait_ge(T.sem["m%d" % (r * NHF + h)], r)
            g.vector.tensor_tensor(T.yb[:, r * TK + h * CW:r * TK + (h + 1) * CW],
                                   T["in%d" % r][:, h * CW:(h + 1) * CW], bank(r, h),
                                   AluOpType.subtract).then_inc(T.sem.yv, 1)
    for h in range(NHF):
        qu = queues[h % 2]
        qu.wait_ge(T.sem.yv, nth(R, h))
        qu.dma_start(T.y[:, h * CW:(h + 1) * CW],
                     T.yb[:, R * TK + h * CW:R * TK + (h + 1) * CW]).then_inc(T.sem["sto%d" % h], 16)
    for h in range(NHF):
        queues[h % 2].wait_ge(T.sem["sto%d" % h], 16)
